import numpy as np
import ml_dtypes


def mxq(x, axis, fmt="e4m3"):
    dtype, down = {"e4m3": (ml_dtypes.float8_e4m3fn, 7), "e5m2": (ml_dtypes.float8_e5m2, 14)}[fmt]
    v = np.moveaxis(np.asarray(x, np.float32).astype(ml_dtypes.bfloat16).astype(np.float64), axis, -1)
    blocks = v.reshape(v.shape[:-1] + (-1, 32))
    amax = np.abs(blocks).max(-1, keepdims=True)
    byte = np.maximum(np.where(amax > 0, np.frexp(amax)[1] - 1 + 127, 0) - down, 1)
    scale = np.exp2(byte - 127.0)
    codes = (blocks / scale).astype(np.float32).astype(dtype).astype(np.float64)
    return np.moveaxis((codes * scale).reshape(v.shape), -1, axis)


WIDE = False


def mx_kscale(k):
    if not WIDE:
        return np.ones(k)
    levels = np.array([10, -10, 5, -5, 0])
    if k % 512:
        return np.exp2(np.random.permutation(np.resize(levels, k // 32))).repeat(32)
    a = np.empty((k // 512, 16))
    for p in range(k // 512):
        a[p, :8] = np.random.permutation(np.resize(levels, 8))
        for g in range(8):
            far = levels[np.abs(levels - a[p, g]) >= 10]
            a[p, g + 8] = far[np.random.randint(len(far))]
    return np.exp2(a.ravel()).repeat(32)


def f64(x):
    return np.asarray(x).astype(np.float64)


def striped(idx):
    return np.tile(idx.reshape(-1, 16).T, (8, 1)).astype(np.uint16)


def unstriped(offs):
    return offs[:16].T.reshape(-1).astype(np.int64)


E2M1 = np.array([0.0, 0.5, 1.0, 1.5, 2.0, 3.0, 4.0, 6.0, -0.0, -0.5, -1.0, -1.5, -2.0, -3.0, -4.0, -6.0])


def pack_weight(w, fmt):
    k, n = w.shape
    w = f64(np.asarray(w, np.float32).astype(ml_dtypes.bfloat16)).reshape(k // 32, 32, n)
    amax = np.abs(w).max(1)
    if fmt == "e4m3":
        byte = np.frexp(amax)[1] - 1 + 127 - 7
    else:
        mant, ex = np.frexp(amax / 6.0)
        byte = np.where(mant > 0.5, ex, ex - 1) + 127
    byte = np.clip(np.where(amax > 0, byte, 1), 1, 254)
    scaled = (w * np.exp2(127.0 - byte)[:, None, :]).reshape(k, n).astype(np.float32)
    by_word = np.ascontiguousarray(scaled.reshape(k // 512, 128, 4, n).transpose(0, 1, 3, 2))
    if fmt == "e4m3":
        words = by_word.astype(ml_dtypes.float8_e4m3fn).view(np.uint8)
    else:
        c = by_word.astype(ml_dtypes.float4_e2m1fn).view(np.uint8) & 0xF
        words = (c[..., 0::2] | (c[..., 1::2] << 4)).reshape(k // 512, 128, 2 * n)
    return np.ascontiguousarray(words), np.ascontiguousarray(byte.astype(np.uint8).reshape(k // 512, 16, n))


def unpack_weight(words, scales, fmt):
    g, _, n = scales.shape
    words = np.ascontiguousarray(words).reshape(g, 128, n, -1)
    if fmt == "e4m3":
        vals = words.view(ml_dtypes.float8_e4m3fn).astype(np.float64)
    else:
        nib = np.empty((g, 128, n, 4), np.uint8)
        nib[..., 0::2] = words & 0xF
        nib[..., 1::2] = words >> 4
        vals = E2M1[nib]
    vals = vals * np.repeat(np.exp2(scales.astype(np.float64) - 127.0), 8, axis=1)[..., None]
    return vals.transpose(0, 1, 3, 2).reshape(g * 512, n)


def gelu(v):
    return 0.5 * v * (1.0 + np.tanh(np.sqrt(2.0 / np.pi) * (v + 0.044715 * v**3)))


K, H, T, S, T3, S2, P = 512, 1024, 4096, 1024, 1024, 512, 512

def setup_inputs():
    n = np.random.standard_normal
    s = mx_kscale(K)[:, None]
    u = mx_kscale(H)[:, None]
    tab_words, tab_scales = pack_weight(n((K, T)) * s, "e4m3")
    tab2_words, tab2_scales = pack_weight(n((H, T3)) / np.sqrt(H) / u, "e4m3")
    w2_words, w2_scales = pack_weight(n((K, H)) / np.sqrt(K) / s, "e2m1")
    return {
        "tab_words": tab_words, "tab_scales": tab_scales,
        "offs": striped(np.random.permutation(T)[:S]),
        "tab2_words": tab2_words, "tab2_scales": tab2_scales,
        "offs2": striped(np.random.permutation(T3)[:S2]),
        "pos1": striped(np.random.permutation(S)[:P]),
        "pos2": striped(np.random.permutation(S)[:P]),
        "w1": (n((K, H)) / np.sqrt(K) / s).astype(np.float32),
        "w2_words": w2_words, "w2_scales": w2_scales,
        "w3": (1.5 * n((K, H)) / np.sqrt(K) / s).astype(np.float32),
        "gain": (1.3 * np.exp(0.3 * n(H)) * u[:, 0]).astype(np.float32),
        "prior": n(S2).astype(np.float32),
    }

def reference(tab_words, tab_scales, offs, tab2_words, tab2_scales, offs2, pos1, pos2, w1, w2_words, w2_scales, w3, gain, prior):
    v = unpack_weight(tab_words, tab_scales, "e4m3")[:, unstriped(offs)]
    v2 = unpack_weight(tab2_words, tab2_scales, "e4m3")[:, unstriped(offs2)]
    w2 = unpack_weight(w2_words, w2_scales, "e2m1")
    a = mxq(f64(w1), 0, "e4m3").T @ v
    b = w2.T @ v
    d = mxq(f64(w3), 0, "e4m3").T @ v
    h = np.maximum(a, b) * np.tanh(d) * f64(gain)[:, None]
    x1 = mxq(h[:, unstriped(pos1)], 0, "e4m3")
    x2 = mxq(np.abs(h[:, unstriped(pos2)]), 0, "e4m3")
    e = v2.T @ x1 + v2.T @ x2
    return e + f64(prior)[:, None]

@@ -1,0 +1,227 @@
+from contextlib import ExitStack
+
+import concourse.mybir as mybir
+
+K, H, T, S, T3, S2, NP = 512, 1024, 4096, 1024, 1024, 512, 512
+FLOPS = 2 * (3 * K * H * S + 2 * H * S2 * NP)
+
+F32 = mybir.dt.float32
+BF16 = mybir.dt.bfloat16
+I32 = mybir.dt.int32
+U32 = mybir.dt.uint32
+U16 = mybir.dt.uint16
+U8 = mybir.dt.uint8
+FP8X4 = mybir.dt.float8_e4m3fn_x4
+FP4X4 = mybir.dt.float4_e2m1fn_x4
+ALU = mybir.AluOpType
+ACT = mybir.ActivationFunctionType
+
+P = 128
+PACK = 4
+KP = P * PACK
+PASSES = H // KP
+BANK = 512
+
+
+def tile_list_technique_suggestion_scores_kernel(
+    tc, tab_words, tab_scales, offs, tab2_words, tab2_scales, offs2, pos1, pos2,
+    w1, w2_words, w2_scales, w3, gain, prior, out,
+):
+    nc = tc.nc
+    with ExitStack() as ctx:
+        keep = ctx.enter_context(tc.tile_pool(name="keep", bufs=1))
+        ring = ctx.enter_context(tc.tile_pool(name="ring", bufs=3))
+        psum = ctx.enter_context(tc.psum_pool(name="psum", bufs=1))
+
+        def held(shape, dtype, name):
+            return keep.tile(shape, dtype, name=name, align_bytes=64)
+
+        offs_t = held([P, S // 16], U16, "offs_t")
+        offs2_t = held([P, S2 // 16], U16, "offs2_t")
+        pos_t = [held([P, NP // 16], U16, "pos%d_t" % x) for x in range(2)]
+        tabw = held([P, T], I32, "tabw")
+        tabs = held([P, T // 4], I32, "tabs")
+        tab2w = [held([P, T3], I32, "tab2w%d" % a) for a in range(PASSES)]
+        tab2s = held([P, T3 // 4], I32, "tab2s")
+        w2w_raw = held([P, H // 2], I32, "w2w_raw")
+        w2s_raw = held([P, H // 4], I32, "w2s_raw")
+        w_raw = [[held([P, PACK, KP], F32, "w_raw%d%d" % (w, a)) for a in range(PASSES)] for w in range(2)]
+        gain_t = held([P, PASSES, PACK], F32, "gain_t")
+        prior_t = held([P, S2 // P], F32, "prior_t")
+
+        nc.vector.memset(w2s_raw[:], 0)
+        nc.vector.memset(tabs[:], 0)
+        nc.gpsimd.memset(tab2s[:], 0)
+
+        def load_w(w, a):
+            src = (w1, w3)[w]
+            nc.sync.dma_start(out=w_raw[w][a][:], in_=src[:, a * KP:(a + 1) * KP].rearrange("(p j) c -> p j c", j=PACK))
+
+        def load_tab2(a):
+            nc.sync.dma_start(out=tab2w[a][:], in_=tab2_words[a].rearrange("p t i -> p (t i)").bitcast(I32))
+
+        nc.sync.dma_start(out=w2w_raw[:], in_=w2_words[0].bitcast(I32))
+        nc.sync.dma_start(out=tabw[:], in_=tab_words[0].rearrange("p t i -> p (t i)").bitcast(I32))
+        for q in range(4):
+            nc.sync.dma_start(out=w2s_raw[32 * q:32 * q + 4, :], in_=w2_scales[0, 4 * q:4 * q + 4, :].bitcast(I32))
+        nc.sync.dma_start(offs_t[:], offs)
+        for q in range(4):
+            nc.sync.dma_start(out=tabs[32 * q:32 * q + 4, :], in_=tab_scales[0, 4 * q:4 * q + 4, :].bitcast(I32))
+        load_w(0, 0)
+        load_w(1, 0)
+        nc.sync.dma_start(pos_t[0][:], pos1)
+        nc.sync.dma_start(pos_t[1][:], pos2)
+        nc.sync.dma_start(offs2_t[:], offs2)
+        load_tab2(0)
+        load_w(0, 1)
+        load_w(1, 1)
+        load_tab2(1)
+        for q in range(4):
+            nc.sync.dma_start(out=tab2s[32 * q:32 * q + 4 * PASSES, :], in_=tab2_scales[:, 4 * q:4 * q + 4, :].bitcast(I32))
+        with nc.allow_non_contiguous_dma(reason="one value of prior to a partition"):
+            nc.sync.dma_start(out=prior_t[:], in_=prior.rearrange("(j p) -> p j", p=P))
+        nc.gpsimd.dma_start(out=gain_t[:], in_=gain.rearrange("(a p t) -> p a t", p=P, t=PACK))
+
+        two = held([P, PASSES, PACK], F32, "two")
+        sgn = held([P, PASSES, PACK], F32, "sgn")
+        mag = held([P, PASSES, PACK], F32, "mag")
+        nc.gpsimd.tensor_scalar(two[:], gain_t[:], 0.0, 2.0, ALU.is_ge, ALU.mult)
+        nc.gpsimd.tensor_scalar(sgn[:], two[:], 1.0, -1.0, ALU.mult, ALU.add)
+        nc.gpsimd.tensor_tensor(mag[:], gain_t[:], sgn[:], ALU.mult)
+
+        w2w = [held([P, PACK, P, 2], U8, "w2w%d" % a) for a in range(PASSES)]
+        w2s = [held([P, PACK, P], U8, "w2s%d" % a) for a in range(PASSES)]
+        for a in range(PASSES):
+            src = w2w_raw[:, a * KP // 2:(a + 1) * KP // 2].bitcast(U8)
+            nc.vector.tensor_copy(out=w2w[a][:].rearrange("p t m b -> p m t b"),
+                                  in_=src.rearrange("p (m t b) -> p m t b", t=PACK, b=2))
+        for a in range(PASSES):
+            src = w2s_raw[:, a * KP // 4:(a + 1) * KP // 4].bitcast(U8)
+            nc.vector.tensor_copy(out=w2s[a][:].rearrange("p t m -> p m t"),
+                                  in_=src.rearrange("p (m t) -> p m t", t=PACK))
+
+        vw = [held([P, BANK], U32, "vw%d" % c) for c in range(2)]
+        vs = [held([P, BANK], U8, "vs%d" % c) for c in range(2)]
+
+        def gather_tab(c):
+            cut = offs_t[:, c * 32:(c + 1) * 32]
+            nc.vector.tensor_copy(vw[c][:], tabw[:].bitcast(U32).indirect(cut))
+            nc.vector.tensor_copy(vs[c][:], tabs[:].bitcast(U8).indirect(cut))
+
+        v2w = [held([P, S2], U32, "v2w%d" % a) for a in range(PASSES)]
+        v2s = held([P, S2], U8, "v2s")
+
+        w_bf = [[held([P, PACK, P, PACK], BF16, "w_bf%d%d" % (w, a)) for a in range(PASSES)] for w in range(2)]
+        wq = [[held([P, KP], U32, "wq%d%d" % (w, a)) for a in range(PASSES)] for w in range(2)]
+        ws = [[held([P, KP], U8, "ws%d%d" % (w, a)) for a in range(PASSES)] for w in range(2)]
+
+        def weave_w(w, a, m0, m1, on_vector):
+            dst = w_bf[w][a][:, :, m0:m1, :].rearrange("p t m j -> p m j t")
+            src = w_raw[w][a][:, :, PACK * m0:PACK * m1].rearrange("p j (m t) -> p m j t", t=PACK)
+            if on_vector:
+                nc.vector.tensor_copy(out=dst, in_=src)
+            else:
+                nc.scalar.copy(out=dst, in_=src)
+
+        def quant_w(w, a):
+            nc.vector.quantize_mx(out=wq[w][a][:].bitcast(FP8X4), scales=ws[w][a][:],
+                                  in_=w_bf[w][a][:].rearrange("p t m j -> p (t m j)"))
+
+        gather_tab(0)
+        weave_w(0, 0, 0, P, False)
+        quant_w(0, 0)
+        weave_w(1, 0, 0, P // 2, True)
+        weave_w(1, 0, P // 2, P, False)
+        quant_w(1, 0)
+        gather_tab(1)
+
+        picked = [[held([P, PACK, NP], F32, "picked%d%d" % (a, x)) for x in range(2)] for a in range(PASSES)]
+        x_bf = [[held([P, NP, PACK], BF16, "x_bf%d%d" % (a, x)) for x in range(2)] for a in range(PASSES)]
+        xq = [[held([P, NP], U32, "xq%d%d" % (a, x)) for x in range(2)] for a in range(PASSES)]
+        xs = [[held([P, NP], U8, "xs%d%d" % (a, x)) for x in range(2)] for a in range(PASSES)]
+        h_tiles = {}
+
+        def first_stage(i):
+            a, t = divmod(i, PACK)
+            cols = slice(t * P, (t + 1) * P)
+            h = ring.tile([P, S], F32, name="h", align_bytes=64)
+            h_tiles[i] = h
+            for c in range(2):
+                pa = psum.tile([P, BANK], F32, name="pa", tag="a%d" % c)
+                pb = psum.tile([P, BANK], F32, name="pb", tag="b%d" % c)
+                pd = psum.tile([P, BANK], F32, name="pd", tag="d%d" % c)
+                rhs = vw[c][:].bitcast(FP8X4)
+                nc.tensor.matmul_mx(out=pb[:], lhsT=w2w[a][:, t].rearrange("p m b -> p (m b)").bitcast(FP4X4),
+                                    lhsT_scale=w2s[a][:, t], rhs=rhs, rhs_scale=vs[c][:], start=True, stop=True)
+                nc.tensor.matmul_mx(out=pa[:], lhsT=wq[0][a][:, cols].bitcast(FP8X4), lhsT_scale=ws[0][a][:, cols],
+                                    rhs=rhs, rhs_scale=vs[c][:], start=True, stop=True)
+                nc.tensor.matmul_mx(out=pd[:], lhsT=wq[1][a][:, cols].bitcast(FP8X4), lhsT_scale=ws[1][a][:, cols],
+                                    rhs=rhs, rhs_scale=vs[c][:], start=True, stop=True)
+                bs = w_raw[0][0][:, (2 * i + c) % PACK, :]
+                if c == 0 and i > 0:
+                    th = picked[(i - 1) // PACK][0][:, (i - 1) % PACK, :]
+                else:
+                    th = ring.tile([P, BANK], F32, name="th")[:]
+                mx = ring.tile([P, BANK], F32, name="mx")
+                nc.scalar.activation(bs, pb[:], ACT.Copy, scale=mag[:, a, t:t + 1])
+                nc.scalar.activation(th, pd[:], ACT.Tanh, scale=sgn[:, a, t:t + 1])
+                nc.vector.scalar_tensor_tensor(mx[:], pa[:], mag[:, a, t:t + 1], bs, ALU.mult, ALU.max)
+                nc.gpsimd.tensor_tensor(h[:, c * BANK:(c + 1) * BANK], mx[:], th, ALU.mult)
+
+        def pick(i):
+            a, t = divmod(i, PACK)
+            for x in (1, 0):
+                nc.vector.tensor_copy(picked[a][x][:, t, :], h_tiles[i][:].indirect(pos_t[x][:]))
+
+        def weave_x(a, x, n0, n1, on_vector):
+            dst = x_bf[a][x][:, n0:n1, :].rearrange("p (c i) t -> p c t i", i=4)
+            src = picked[a][x][:, :, n0:n1].rearrange("p t (c i) -> p c t i", i=4)
+            if on_vector:
+                nc.vector.tensor_copy(out=dst, in_=src)
+            else:
+                nc.scalar.activation(dst, src, ACT.Abs if x == 1 else ACT.Copy)
+
+        def quant_x(a, x):
+            nc.vector.quantize_mx(out=xq[a][x][:].bitcast(FP8X4), scales=xs[a][x][:],
+                                  in_=x_bf[a][x][:].rearrange("p n t -> p (n t)"))
+
+        for i in range(PASSES * PACK):
+            first_stage(i)
+            if i >= 1:
+                pick(i - 1)
+            if i == 0:
+                nc.vector.tensor_copy(v2w[0][:], tab2w[0][:].bitcast(U32).indirect(offs2_t[:]))
+            if i in (0, 1):
+                for u in range(4):
+                    weave_w(i, 1, u * P // 4, (u + 1) * P // 4, False)
+                quant_w(i, 1)
+            if i in (4, 5):
+                for u in range(4):
+                    weave_x(0, 5 - i, u * NP // 4, (u + 1) * NP // 4, False)
+                quant_x(0, 5 - i)
+            if i == 4:
+                nc.vector.tensor_copy(v2s[:], tab2s[:].bitcast(U8).indirect(offs2_t[:]))
+            if i == 6:
+                nc.vector.tensor_copy(v2w[1][:], tab2w[1][:].bitcast(U32).indirect(offs2_t[:]))
+        pick(PASSES * PACK - 1)
+        weave_x(1, 1, 0, NP, False)
+        weave_x(1, 0, 0, NP, True)
+        quant_x(1, 0)
+        quant_x(1, 1)
+
+        tags = ("e0", "e1", "b0", "d0")
+        acc = [psum.tile([P, BANK], F32, name="acc%d" % j, tag=tags[j]) for j in range(S2 // P)]
+        steps = ((0, 1), (0, 0), (1, 0), (1, 1))
+        for n, (a, x) in enumerate(steps):
+            for j in range(S2 // P):
+                cols = slice(j * P, (j + 1) * P)
+                nc.tensor.matmul_mx(out=acc[j][:], lhsT=v2w[a][:, cols].bitcast(FP8X4), lhsT_scale=v2s[4 * a:P, cols],
+                                    rhs=xq[a][x][:].bitcast(FP8X4), rhs_scale=xs[a][x][:],
+                                    start=(n == 0), stop=(n == len(steps) - 1))
+        for j in range(S2 // P):
+            res = held([P, NP], F32, "res%d" % j)
+            if j % 2 == 0:
+                nc.scalar.activation(res[:], acc[j][:], ACT.Identity, bias=prior_t[:, j:j + 1])
+            else:
+                nc.vector.tensor_scalar(res[:], acc[j][:], prior_t[:, j:j + 1], None, ALU.add)
+            nc.sync.dma_start(out=out[j * P:(j + 1) * P, :], in_=res[:])

@@ -21,6 +21,9 @@ PACK = 4
 KP = P * PACK
 PASSES = H // KP
 BANK = 512
+LAG = 3
+HOLD = {10: (1, 0), 11: (1, 1), 13: (0, 0), 14: (0, 1)}
+WENG = ("scalar", "scalar", "scalar", "scalar", "scalar", "scalar", "scalar", "scalar")
 
 
 def tile_list_technique_suggestion_scores_kernel(
@@ -49,33 +52,36 @@ def tile_list_technique_suggestion_scores_kernel(
         gain_t = held([P, PASSES, PACK], F32, "gain_t")
         prior_t = held([P, S2 // P], F32, "prior_t")
 
-        nc.vector.memset(w2s_raw[:], 0)
-        nc.vector.memset(tabs[:], 0)
+        nc.gpsimd.memset(w2s_raw[:], 0)
+        nc.gpsimd.memset(tabs[:, T // 8:], 0)
+        nc.vector.memset(tabs[:, :T // 8], 0)
         nc.gpsimd.memset(tab2s[:], 0)
 
-        def load_w(w, a):
+        def load_w(w, a, c0, c1):
             src = (w1, w3)[w]
-            nc.sync.dma_start(out=w_raw[w][a][:], in_=src[:, a * KP:(a + 1) * KP].rearrange("(p j) c -> p j c", j=PACK))
+            nc.sync.dma_start(out=w_raw[w][a][:, :, c0:c1],
+                              in_=src[:, a * KP + c0:a * KP + c1].rearrange("(p j) c -> p j c", j=PACK))
 
         def load_tab2(a):
             nc.sync.dma_start(out=tab2w[a][:], in_=tab2_words[a].rearrange("p t i -> p (t i)").bitcast(I32))
 
         nc.sync.dma_start(out=w2w_raw[:], in_=w2_words[0].bitcast(I32))
-        nc.sync.dma_start(out=tabw[:], in_=tab_words[0].rearrange("p t i -> p (t i)").bitcast(I32))
+        nc.sync.dma_start(offs_t[:], offs)
+        nc.sync.dma_start(pos_t[1][:], pos2)
         for q in range(4):
             nc.sync.dma_start(out=w2s_raw[32 * q:32 * q + 4, :], in_=w2_scales[0, 4 * q:4 * q + 4, :].bitcast(I32))
-        nc.sync.dma_start(offs_t[:], offs)
+        nc.sync.dma_start(out=tabw[:], in_=tab_words[0].rearrange("p t i -> p (t i)").bitcast(I32))
         for q in range(4):
             nc.sync.dma_start(out=tabs[32 * q:32 * q + 4, :], in_=tab_scales[0, 4 * q:4 * q + 4, :].bitcast(I32))
-        load_w(0, 0)
-        load_w(1, 0)
+        for w in range(2):
+            for u in range(2):
+                load_w(w, 0, u * KP // 2, (u + 1) * KP // 2)
         nc.sync.dma_start(pos_t[0][:], pos1)
-        nc.sync.dma_start(pos_t[1][:], pos2)
         nc.sync.dma_start(offs2_t[:], offs2)
         load_tab2(0)
-        load_w(0, 1)
-        load_w(1, 1)
         load_tab2(1)
+        load_w(0, 1, 0, KP)
+        load_w(1, 1, 0, KP)
         for q in range(4):
             nc.sync.dma_start(out=tab2s[32 * q:32 * q + 4 * PASSES, :], in_=tab2_scales[:, 4 * q:4 * q + 4, :].bitcast(I32))
         with nc.allow_non_contiguous_dma(reason="one value of prior to a partition"):
@@ -103,10 +109,10 @@ def tile_list_technique_suggestion_scores_kernel(
         vw = [held([P, BANK], U32, "vw%d" % c) for c in range(2)]
         vs = [held([P, BANK], U8, "vs%d" % c) for c in range(2)]
 
-        def gather_tab(c):
-            cut = offs_t[:, c * 32:(c + 1) * 32]
-            nc.vector.tensor_copy(vw[c][:], tabw[:].bitcast(U32).indirect(cut))
-            nc.vector.tensor_copy(vs[c][:], tabs[:].bitcast(U8).indirect(cut))
+        for c in range(2):
+            nc.vector.tensor_copy(vw[c][:], tabw[:].bitcast(U32).indirect(offs_t[:, c * 32:(c + 1) * 32]))
+        for c in range(2):
+            nc.vector.tensor_copy(vs[c][:], tabs[:].bitcast(U8).indirect(offs_t[:, c * 32:(c + 1) * 32]))
 
         v2w = [held([P, S2], U32, "v2w%d" % a) for a in range(PASSES)]
         v2s = held([P, S2], U8, "v2s")
@@ -115,25 +121,31 @@ def tile_list_technique_suggestion_scores_kernel(
         wq = [[held([P, KP], U32, "wq%d%d" % (w, a)) for a in range(PASSES)] for w in range(2)]
         ws = [[held([P, KP], U8, "ws%d%d" % (w, a)) for a in range(PASSES)] for w in range(2)]
 
-        def weave_w(w, a, m0, m1, on_vector):
-            dst = w_bf[w][a][:, :, m0:m1, :].rearrange("p t m j -> p m j t")
-            src = w_raw[w][a][:, :, PACK * m0:PACK * m1].rearrange("p j (m t) -> p m j t", t=PACK)
-            if on_vector:
+        def round_copy(engine, dst, src):
+            if engine == "vector":
                 nc.vector.tensor_copy(out=dst, in_=src)
+            elif engine == "gpsimd":
+                nc.gpsimd.tensor_scalar(dst, src, 1.0, 0.0, ALU.mult, ALU.add)
             else:
                 nc.scalar.copy(out=dst, in_=src)
 
-        def quant_w(w, a):
-            nc.vector.quantize_mx(out=wq[w][a][:].bitcast(FP8X4), scales=ws[w][a][:],
-                                  in_=w_bf[w][a][:].rearrange("p t m j -> p (t m j)"))
+        def weave_w(w, a, m0, m1, engine):
+            dst = w_bf[w][a][:, :, m0:m1, :].rearrange("p t m j -> p m j t")
+            src = w_raw[w][a][:, :, PACK * m0:PACK * m1].rearrange("p j (m t) -> p m j t", t=PACK)
+            round_copy(engine, dst, src)
 
-        gather_tab(0)
-        weave_w(0, 0, 0, P, False)
-        quant_w(0, 0)
-        weave_w(1, 0, 0, P // 2, True)
-        weave_w(1, 0, P // 2, P, False)
-        quant_w(1, 0)
-        gather_tab(1)
+        def quant_w(w, a, t0, t1):
+            nc.vector.quantize_mx(out=wq[w][a][:, t0 * P:t1 * P].bitcast(FP8X4), scales=ws[w][a][:, t0 * P:t1 * P],
+                                  in_=w_bf[w][a][:, t0:t1].rearrange("p t m j -> p (t m j)"))
+
+        weave_w(0, 0, 0, P // 2, "scalar")
+        weave_w(0, 0, P // 2, P, "scalar")
+        weave_w(1, 0, 0, P // 2, "scalar")
+        quant_w(0, 0, 0, 1)
+        weave_w(1, 0, P // 2, P, "vector")
+        quant_w(0, 0, 1, PACK)
+        quant_w(1, 0, 0, 1)
+        quant_w(1, 0, 1, PACK)
 
         picked = [[held([P, PACK, NP], F32, "picked%d%d" % (a, x)) for x in range(2)] for a in range(PASSES)]
         x_bf = [[held([P, NP, PACK], BF16, "x_bf%d%d" % (a, x)) for x in range(2)] for a in range(PASSES)]
@@ -141,87 +153,132 @@ def tile_list_technique_suggestion_scores_kernel(
         xs = [[held([P, NP], U8, "xs%d%d" % (a, x)) for x in range(2)] for a in range(PASSES)]
         h_tiles = {}
 
-        def first_stage(i):
+        def first_stage(i, c):
             a, t = divmod(i, PACK)
             cols = slice(t * P, (t + 1) * P)
-            h = ring.tile([P, S], F32, name="h", align_bytes=64)
-            h_tiles[i] = h
-            for c in range(2):
-                pa = psum.tile([P, BANK], F32, name="pa", tag="a%d" % c)
-                pb = psum.tile([P, BANK], F32, name="pb", tag="b%d" % c)
-                pd = psum.tile([P, BANK], F32, name="pd", tag="d%d" % c)
-                rhs = vw[c][:].bitcast(FP8X4)
-                nc.tensor.matmul_mx(out=pb[:], lhsT=w2w[a][:, t].rearrange("p m b -> p (m b)").bitcast(FP4X4),
-                                    lhsT_scale=w2s[a][:, t], rhs=rhs, rhs_scale=vs[c][:], start=True, stop=True)
-                nc.tensor.matmul_mx(out=pa[:], lhsT=wq[0][a][:, cols].bitcast(FP8X4), lhsT_scale=ws[0][a][:, cols],
-                                    rhs=rhs, rhs_scale=vs[c][:], start=True, stop=True)
-                nc.tensor.matmul_mx(out=pd[:], lhsT=wq[1][a][:, cols].bitcast(FP8X4), lhsT_scale=ws[1][a][:, cols],
-                                    rhs=rhs, rhs_scale=vs[c][:], start=True, stop=True)
-                bs = w_raw[0][0][:, (2 * i + c) % PACK, :]
-                if c == 0 and i > 0:
-                    th = picked[(i - 1) // PACK][0][:, (i - 1) % PACK, :]
-                else:
-                    th = ring.tile([P, BANK], F32, name="th")[:]
-                mx = ring.tile([P, BANK], F32, name="mx")
-                nc.scalar.activation(bs, pb[:], ACT.Copy, scale=mag[:, a, t:t + 1])
-                nc.scalar.activation(th, pd[:], ACT.Tanh, scale=sgn[:, a, t:t + 1])
-                nc.vector.scalar_tensor_tensor(mx[:], pa[:], mag[:, a, t:t + 1], bs, ALU.mult, ALU.max)
-                nc.gpsimd.tensor_tensor(h[:, c * BANK:(c + 1) * BANK], mx[:], th, ALU.mult)
+            if c == 0:
+                h_tiles[i] = ring.tile([P, S], F32, name="h", align_bytes=64)
+            h = h_tiles[i]
+            pa = psum.tile([P, BANK], F32, name="pa", tag="a%d" % c)
+            pb = psum.tile([P, BANK], F32, name="pb", tag="b%d" % c)
+            pd = psum.tile([P, BANK], F32, name="pd", tag="d%d" % c)
+            rhs = vw[c][:].bitcast(FP8X4)
+            nc.tensor.matmul_mx(out=pb[:], lhsT=w2w[a][:, t].rearrange("p m b -> p (m b)").bitcast(FP4X4),
+                                lhsT_scale=w2s[a][:, t], rhs=rhs, rhs_scale=vs[c][:], start=True, stop=True)
+            nc.tensor.matmul_mx(out=pa[:], lhsT=wq[0][a][:, cols].bitcast(FP8X4), lhsT_scale=ws[0][a][:, cols],
+                                rhs=rhs, rhs_scale=vs[c][:], start=True, stop=True)
+            nc.tensor.matmul_mx(out=pd[:], lhsT=wq[1][a][:, cols].bitcast(FP8X4), lhsT_scale=ws[1][a][:, cols],
+                                rhs=rhs, rhs_scale=vs[c][:], start=True, stop=True)
+            k = 2 * i + c
+            if k >= LAG:
+                tile_no, second = divmod(k - LAG, 2)
+                bs = picked[tile_no // PACK][1 - second][:, tile_no % PACK, :]
+            else:
+                bs = w_raw[0][0][:, k, :]
+            if k in HOLD:
+                x, u = HOLD[k]
+                th = x_bf[0][x][:, u * NP // 2:(u + 1) * NP // 2, :].rearrange("p n t -> p (n t)").bitcast(F32)
+            else:
+                th = ring.tile([P, BANK], F32, name="th")[:]
+            if k == 2 * last + 1:
+                mx = picked[PASSES - 1][0][:, PACK - 2, :]
+            else:
+                mx = ring.tile([P, BANK], F32, name="mx")[:]
+            nc.scalar.activation(bs, pb[:], ACT.Copy, scale=mag[:, a, t:t + 1])
+            nc.scalar.activation(th, pd[:], ACT.Tanh, scale=sgn[:, a, t:t + 1])
+            nc.vector.scalar_tensor_tensor(mx, pa[:], mag[:, a, t:t + 1], bs, ALU.mult, ALU.max)
+            nc.gpsimd.tensor_tensor(h[:, c * BANK:(c + 1) * BANK], mx, th, ALU.mult)
 
-        def pick(i):
+        def pick(i, x, n0, n1):
             a, t = divmod(i, PACK)
-            for x in (1, 0):
-                nc.vector.tensor_copy(picked[a][x][:, t, :], h_tiles[i][:].indirect(pos_t[x][:]))
+            nc.vector.tensor_copy(picked[a][x][:, t, n0:n1], h_tiles[i][:].indirect(pos_t[x][:, n0 // 16:n1 // 16]))
 
-        def weave_x(a, x, n0, n1, on_vector):
+        def weave_x(a, x, n0, n1, engine):
             dst = x_bf[a][x][:, n0:n1, :].rearrange("p (c i) t -> p c t i", i=4)
             src = picked[a][x][:, :, n0:n1].rearrange("p t (c i) -> p c t i", i=4)
-            if on_vector:
-                nc.vector.tensor_copy(out=dst, in_=src)
+            if x == 1:
+                nc.scalar.activation(dst, src, ACT.Abs)
             else:
-                nc.scalar.activation(dst, src, ACT.Abs if x == 1 else ACT.Copy)
+                round_copy(engine, dst, src)
 
-        def quant_x(a, x):
-            nc.vector.quantize_mx(out=xq[a][x][:].bitcast(FP8X4), scales=xs[a][x][:],
-                                  in_=x_bf[a][x][:].rearrange("p n t -> p (n t)"))
+        def quant_x(a, x, n0, n1):
+            nc.vector.quantize_mx(out=xq[a][x][:, n0:n1].bitcast(FP8X4), scales=xs[a][x][:, n0:n1],
+                                  in_=x_bf[a][x][:, n0:n1].rearrange("p n t -> p (n t)"))
 
+        def finish(k):
+            if k in HOLD:
+                x, u = HOLD[k]
+                for v in (2 * u, 2 * u + 1):
+                    weave_x(0, x, v * NP // 4, (v + 1) * NP // 4, "scalar")
+                if u == 1:
+                    quant_x(0, x, 0, NP)
+
+        last = PASSES * PACK - 1
         for i in range(PASSES * PACK):
-            first_stage(i)
-            if i >= 1:
-                pick(i - 1)
-            if i == 0:
-                nc.vector.tensor_copy(v2w[0][:], tab2w[0][:].bitcast(U32).indirect(offs2_t[:]))
-            if i in (0, 1):
-                for u in range(4):
-                    weave_w(i, 1, u * P // 4, (u + 1) * P // 4, False)
-                quant_w(i, 1)
-            if i in (4, 5):
-                for u in range(4):
-                    weave_x(0, 5 - i, u * NP // 4, (u + 1) * NP // 4, False)
-                quant_x(0, 5 - i)
-            if i == 4:
-                nc.vector.tensor_copy(v2s[:], tab2s[:].bitcast(U8).indirect(offs2_t[:]))
-            if i == 6:
-                nc.vector.tensor_copy(v2w[1][:], tab2w[1][:].bitcast(U32).indirect(offs2_t[:]))
-        pick(PASSES * PACK - 1)
-        weave_x(1, 1, 0, NP, False)
-        weave_x(1, 0, 0, NP, True)
-        quant_x(1, 0)
-        quant_x(1, 1)
+            for c in range(2):
+                k = 2 * i + c
+                first_stage(i, c)
+                if k >= LAG:
+                    pick((k - LAG) // 2, 1 - (k - LAG) % 2, 0, NP)
+                if k == 0:
+                    nc.vector.tensor_copy(v2w[0][:], tab2w[0][:].bitcast(U32).indirect(offs2_t[:]))
+                if 1 <= k <= 4:
+                    w, u = divmod(k - 1, 2)
+                    for v in (2 * u, 2 * u + 1):
+                        weave_w(w, 1, v * P // 4, (v + 1) * P // 4, WENG[4 * w + v])
+                    if u == 1:
+                        quant_w(w, 1, 0, PACK)
+                if k == 3:
+                    nc.vector.tensor_copy(v2w[1][:], tab2w[1][:].bitcast(U32).indirect(offs2_t[:]))
+                if k == 5:
+                    nc.vector.tensor_copy(v2s[:], tab2s[:].bitcast(U8).indirect(offs2_t[:]))
+                finish(k - 2)
+        for k in range(2 * last + 2 - 2, 2 * last + 2):
+            finish(k)
+        for job in range(2 * last + 2 - LAG, 2 * last):
+            pick(job // 2, 1 - job % 2, 0, NP)
+        half = NP // 2
+        pick(last, 0, 0, half)
+        weave_x(1, 0, 0, half, "scalar")
+        pick(last, 1, 0, half)
+        weave_x(1, 1, 0, half, "scalar")
+        pick(last, 0, half, NP)
+        pick(last, 1, half, NP)
+        weave_x(1, 1, half, NP, "scalar")
+        weave_x(1, 0, half, NP, "vector")
+        quant_x(1, 0, 0, half)
+        quant_x(1, 1, 0, half)
+        quant_x(1, 0, half, NP)
+        quant_x(1, 1, half, NP)
 
-        tags = ("e0", "e1", "b0", "d0")
-        acc = [psum.tile([P, BANK], F32, name="acc%d" % j, tag=tags[j]) for j in range(S2 // P)]
+        tags = ("b0", "d0", "d1", "a1")
+        acc = [psum.tile([P, 2, half], F32, name="acc%d" % g, tag=tags[g]) for g in range(4)]
         steps = ((0, 1), (0, 0), (1, 0), (1, 1))
-        for n, (a, x) in enumerate(steps):
-            for j in range(S2 // P):
+
+        def second_stage(g, n):
+            a, x = steps[n]
+            ns = slice((g // 2) * half, (g // 2 + 1) * half)
+            for u in range(2):
+                j = 2 * (g % 2) + u
                 cols = slice(j * P, (j + 1) * P)
-                nc.tensor.matmul_mx(out=acc[j][:], lhsT=v2w[a][:, cols].bitcast(FP8X4), lhsT_scale=v2s[4 * a:P, cols],
-                                    rhs=xq[a][x][:].bitcast(FP8X4), rhs_scale=xs[a][x][:],
-                                    start=(n == 0), stop=(n == len(steps) - 1))
-        for j in range(S2 // P):
-            res = held([P, NP], F32, "res%d" % j)
-            if j % 2 == 0:
-                nc.scalar.activation(res[:], acc[j][:], ACT.Identity, bias=prior_t[:, j:j + 1])
-            else:
-                nc.vector.tensor_scalar(res[:], acc[j][:], prior_t[:, j:j + 1], None, ALU.add)
-            nc.sync.dma_start(out=out[j * P:(j + 1) * P, :], in_=res[:])
+                nc.tensor.matmul_mx(out=acc[g][:, u, :], lhsT=v2w[a][:, cols].bitcast(FP8X4), lhsT_scale=v2s[4 * a:P, cols],
+                                    rhs=xq[a][x][:, ns].bitcast(FP8X4), rhs_scale=xs[a][x][:, ns],
+                                    start=(n == 0 and u == 0), stop=(n == len(steps) - 1 and u == 1))
+
+        for g in range(4):
+            for n in range(2):
+                second_stage(g, n)
+        for g0 in (0, 2):
+            for n in (2, 3):
+                for g in (g0, g0 + 1):
+                    second_stage(g, n)
+        for g in range(4):
+            res = held([P, 2, half], F32, "res%d" % g)
+            for u in range(2):
+                j = 2 * (g % 2) + u
+                if g % 2 == 0:
+                    nc.scalar.activation(res[:, u, :], acc[g][:, u, :], ACT.Identity, bias=prior_t[:, j:j + 1])
+                else:
+                    nc.vector.tensor_scalar(res[:, u, :], acc[g][:, u, :], prior_t[:, j:j + 1], None, ALU.add)
+            rows = out[2 * (g % 2) * P:2 * (g % 2 + 1) * P, (g // 2) * half:(g // 2 + 1) * half]
+            nc.sync.dma_start(out=rows.rearrange("(u p) n -> p u n", p=P), in_=res[:])

from contextlib import ExitStack

import concourse.mybir as mybir

K, H, T, S, T3, S2, NP = 512, 1024, 4096, 1024, 1024, 512, 512
FLOPS = 2 * (3 * K * H * S + 2 * H * S2 * NP)

F32 = mybir.dt.float32
BF16 = mybir.dt.bfloat16
I32 = mybir.dt.int32
U32 = mybir.dt.uint32
U16 = mybir.dt.uint16
U8 = mybir.dt.uint8
FP8X4 = mybir.dt.float8_e4m3fn_x4
FP4X4 = mybir.dt.float4_e2m1fn_x4
ALU = mybir.AluOpType
ACT = mybir.ActivationFunctionType

P = 128
PACK = 4
KP = P * PACK
PASSES = H // KP
BANK = 512
LAG = 3
HOLD = {10: (1, 0), 11: (1, 1), 13: (0, 0), 14: (0, 1)}
WENG = ("scalar", "scalar", "scalar", "scalar", "scalar", "scalar", "scalar", "scalar")


def tile_list_technique_suggestion_scores_kernel(
    tc, tab_words, tab_scales, offs, tab2_words, tab2_scales, offs2, pos1, pos2,
    w1, w2_words, w2_scales, w3, gain, prior, out,
):
    nc = tc.nc
    with ExitStack() as ctx:
        keep = ctx.enter_context(tc.tile_pool(name="keep", bufs=1))
        ring = ctx.enter_context(tc.tile_pool(name="ring", bufs=3))
        psum = ctx.enter_context(tc.psum_pool(name="psum", bufs=1))

        def held(shape, dtype, name):
            return keep.tile(shape, dtype, name=name, align_bytes=64)

        offs_t = held([P, S // 16], U16, "offs_t")
        offs2_t = held([P, S2 // 16], U16, "offs2_t")
        pos_t = [held([P, NP // 16], U16, "pos%d_t" % x) for x in range(2)]
        tabw = held([P, T], I32, "tabw")
        tabs = held([P, T // 4], I32, "tabs")
        tab2w = [held([P, T3], I32, "tab2w%d" % a) for a in range(PASSES)]
        tab2s = held([P, T3 // 4], I32, "tab2s")
        w2w_raw = held([P, H // 2], I32, "w2w_raw")
        w2s_raw = held([P, H // 4], I32, "w2s_raw")
        w_raw = [[held([P, PACK, KP], F32, "w_raw%d%d" % (w, a)) for a in range(PASSES)] for w in range(2)]
        gain_t = held([P, PASSES, PACK], F32, "gain_t")
        prior_t = held([P, S2 // P], F32, "prior_t")

        nc.gpsimd.memset(w2s_raw[:], 0)
        nc.gpsimd.memset(tabs[:, T // 8:], 0)
        nc.vector.memset(tabs[:, :T // 8], 0)
        nc.gpsimd.memset(tab2s[:], 0)

        def load_w(w, a, c0, c1):
            src = (w1, w3)[w]
            nc.sync.dma_start(out=w_raw[w][a][:, :, c0:c1],
                              in_=src[:, a * KP + c0:a * KP + c1].rearrange("(p j) c -> p j c", j=PACK))

        def load_tab2(a):
            nc.sync.dma_start(out=tab2w[a][:], in_=tab2_words[a].rearrange("p t i -> p (t i)").bitcast(I32))

        nc.sync.dma_start(out=w2w_raw[:], in_=w2_words[0].bitcast(I32))
        nc.sync.dma_start(offs_t[:], offs)
        nc.sync.dma_start(pos_t[1][:], pos2)
        for q in range(4):
            nc.sync.dma_start(out=w2s_raw[32 * q:32 * q + 4, :], in_=w2_scales[0, 4 * q:4 * q + 4, :].bitcast(I32))
        nc.sync.dma_start(out=tabw[:], in_=tab_words[0].rearrange("p t i -> p (t i)").bitcast(I32))
        for q in range(4):
            nc.sync.dma_start(out=tabs[32 * q:32 * q + 4, :], in_=tab_scales[0, 4 * q:4 * q + 4, :].bitcast(I32))
        for w in range(2):
            for u in range(2):
                load_w(w, 0, u * KP // 2, (u + 1) * KP // 2)
        nc.sync.dma_start(pos_t[0][:], pos1)
        nc.sync.dma_start(offs2_t[:], offs2)
        load_tab2(0)
        load_tab2(1)
        load_w(0, 1, 0, KP)
        load_w(1, 1, 0, KP)
        for q in range(4):
            nc.sync.dma_start(out=tab2s[32 * q:32 * q + 4 * PASSES, :], in_=tab2_scales[:, 4 * q:4 * q + 4, :].bitcast(I32))
        with nc.allow_non_contiguous_dma(reason="one value of prior to a partition"):
            nc.sync.dma_start(out=prior_t[:], in_=prior.rearrange("(j p) -> p j", p=P))
        nc.gpsimd.dma_start(out=gain_t[:], in_=gain.rearrange("(a p t) -> p a t", p=P, t=PACK))

        two = held([P, PASSES, PACK], F32, "two")
        sgn = held([P, PASSES, PACK], F32, "sgn")
        mag = held([P, PASSES, PACK], F32, "mag")
        nc.gpsimd.tensor_scalar(two[:], gain_t[:], 0.0, 2.0, ALU.is_ge, ALU.mult)
        nc.gpsimd.tensor_scalar(sgn[:], two[:], 1.0, -1.0, ALU.mult, ALU.add)
        nc.gpsimd.tensor_tensor(mag[:], gain_t[:], sgn[:], ALU.mult)

        w2w = [held([P, PACK, P, 2], U8, "w2w%d" % a) for a in range(PASSES)]
        w2s = [held([P, PACK, P], U8, "w2s%d" % a) for a in range(PASSES)]
        for a in range(PASSES):
            src = w2w_raw[:, a * KP // 2:(a + 1) * KP // 2].bitcast(U8)
            nc.vector.tensor_copy(out=w2w[a][:].rearrange("p t m b -> p m t b"),
                                  in_=src.rearrange("p (m t b) -> p m t b", t=PACK, b=2))
        for a in range(PASSES):
            src = w2s_raw[:, a * KP // 4:(a + 1) * KP // 4].bitcast(U8)
            nc.vector.tensor_copy(out=w2s[a][:].rearrange("p t m -> p m t"),
                                  in_=src.rearrange("p (m t) -> p m t", t=PACK))

        vw = [held([P, BANK], U32, "vw%d" % c) for c in range(2)]
        vs = [held([P, BANK], U8, "vs%d" % c) for c in range(2)]

        for c in range(2):
            nc.vector.tensor_copy(vw[c][:], tabw[:].bitcast(U32).indirect(offs_t[:, c * 32:(c + 1) * 32]))
        for c in range(2):
            nc.vector.tensor_copy(vs[c][:], tabs[:].bitcast(U8).indirect(offs_t[:, c * 32:(c + 1) * 32]))

        v2w = [held([P, S2], U32, "v2w%d" % a) for a in range(PASSES)]
        v2s = held([P, S2], U8, "v2s")

        w_bf = [[held([P, PACK, P, PACK], BF16, "w_bf%d%d" % (w, a)) for a in range(PASSES)] for w in range(2)]
        wq = [[held([P, KP], U32, "wq%d%d" % (w, a)) for a in range(PASSES)] for w in range(2)]
        ws = [[held([P, KP], U8, "ws%d%d" % (w, a)) for a in range(PASSES)] for w in range(2)]

        def round_copy(engine, dst, src):
            if engine == "vector":
                nc.vector.tensor_copy(out=dst, in_=src)
            elif engine == "gpsimd":
                nc.gpsimd.tensor_scalar(dst, src, 1.0, 0.0, ALU.mult, ALU.add)
            else:
                nc.scalar.copy(out=dst, in_=src)

        def weave_w(w, a, m0, m1, engine):
            dst = w_bf[w][a][:, :, m0:m1, :].rearrange("p t m j -> p m j t")
            src = w_raw[w][a][:, :, PACK * m0:PACK * m1].rearrange("p j (m t) -> p m j t", t=PACK)
            round_copy(engine, dst, src)

        def quant_w(w, a, t0, t1):
            nc.vector.quantize_mx(out=wq[w][a][:, t0 * P:t1 * P].bitcast(FP8X4), scales=ws[w][a][:, t0 * P:t1 * P],
                                  in_=w_bf[w][a][:, t0:t1].rearrange("p t m j -> p (t m j)"))

        weave_w(0, 0, 0, P // 2, "scalar")
        weave_w(0, 0, P // 2, P, "scalar")
        weave_w(1, 0, 0, P // 2, "scalar")
        quant_w(0, 0, 0, 1)
        weave_w(1, 0, P // 2, P, "vector")
        quant_w(0, 0, 1, PACK)
        quant_w(1, 0, 0, 1)
        quant_w(1, 0, 1, PACK)

        picked = [[held([P, PACK, NP], F32, "picked%d%d" % (a, x)) for x in range(2)] for a in range(PASSES)]
        x_bf = [[held([P, NP, PACK], BF16, "x_bf%d%d" % (a, x)) for x in range(2)] for a in range(PASSES)]
        xq = [[held([P, NP], U32, "xq%d%d" % (a, x)) for x in range(2)] for a in range(PASSES)]
        xs = [[held([P, NP], U8, "xs%d%d" % (a, x)) for x in range(2)] for a in range(PASSES)]
        h_tiles = {}

        def first_stage(i, c):
            a, t = divmod(i, PACK)
            cols = slice(t * P, (t + 1) * P)
            if c == 0:
                h_tiles[i] = ring.tile([P, S], F32, name="h", align_bytes=64)
            h = h_tiles[i]
            pa = psum.tile([P, BANK], F32, name="pa", tag="a%d" % c)
            pb = psum.tile([P, BANK], F32, name="pb", tag="b%d" % c)
            pd = psum.tile([P, BANK], F32, name="pd", tag="d%d" % c)
            rhs = vw[c][:].bitcast(FP8X4)
            nc.tensor.matmul_mx(out=pb[:], lhsT=w2w[a][:, t].rearrange("p m b -> p (m b)").bitcast(FP4X4),
                                lhsT_scale=w2s[a][:, t], rhs=rhs, rhs_scale=vs[c][:], start=True, stop=True)
            nc.tensor.matmul_mx(out=pa[:], lhsT=wq[0][a][:, cols].bitcast(FP8X4), lhsT_scale=ws[0][a][:, cols],
                                rhs=rhs, rhs_scale=vs[c][:], start=True, stop=True)
            nc.tensor.matmul_mx(out=pd[:], lhsT=wq[1][a][:, cols].bitcast(FP8X4), lhsT_scale=ws[1][a][:, cols],
                                rhs=rhs, rhs_scale=vs[c][:], start=True, stop=True)
            k = 2 * i + c
            if k >= LAG:
                tile_no, second = divmod(k - LAG, 2)
                bs = picked[tile_no // PACK][1 - second][:, tile_no % PACK, :]
            else:
                bs = w_raw[0][0][:, k, :]
            if k in HOLD:
                x, u = HOLD[k]
                th = x_bf[0][x][:, u * NP // 2:(u + 1) * NP // 2, :].rearrange("p n t -> p (n t)").bitcast(F32)
            else:
                th = ring.tile([P, BANK], F32, name="th")[:]
            if k == 2 * last + 1:
                mx = picked[PASSES - 1][0][:, PACK - 2, :]
            else:
                mx = ring.tile([P, BANK], F32, name="mx")[:]
            nc.scalar.activation(bs, pb[:], ACT.Copy, scale=mag[:, a, t:t + 1])
            nc.scalar.activation(th, pd[:], ACT.Tanh, scale=sgn[:, a, t:t + 1])
            nc.vector.scalar_tensor_tensor(mx, pa[:], mag[:, a, t:t + 1], bs, ALU.mult, ALU.max)
            nc.gpsimd.tensor_tensor(h[:, c * BANK:(c + 1) * BANK], mx, th, ALU.mult)

        def pick(i, x, n0, n1):
            a, t = divmod(i, PACK)
            nc.vector.tensor_copy(picked[a][x][:, t, n0:n1], h_tiles[i][:].indirect(pos_t[x][:, n0 // 16:n1 // 16]))

        def weave_x(a, x, n0, n1, engine):
            dst = x_bf[a][x][:, n0:n1, :].rearrange("p (c i) t -> p c t i", i=4)
            src = picked[a][x][:, :, n0:n1].rearrange("p t (c i) -> p c t i", i=4)
            if x == 1:
                nc.scalar.activation(dst, src, ACT.Abs)
            else:
                round_copy(engine, dst, src)

        def quant_x(a, x, n0, n1):
            nc.vector.quantize_mx(out=xq[a][x][:, n0:n1].bitcast(FP8X4), scales=xs[a][x][:, n0:n1],
                                  in_=x_bf[a][x][:, n0:n1].rearrange("p n t -> p (n t)"))

        def finish(k):
            if k in HOLD:
                x, u = HOLD[k]
                for v in (2 * u, 2 * u + 1):
                    weave_x(0, x, v * NP // 4, (v + 1) * NP // 4, "scalar")
                if u == 1:
                    quant_x(0, x, 0, NP)

        last = PASSES * PACK - 1
        for i in range(PASSES * PACK):
            for c in range(2):
                k = 2 * i + c
                first_stage(i, c)
                if k >= LAG:
                    pick((k - LAG) // 2, 1 - (k - LAG) % 2, 0, NP)
                if k == 0:
                    nc.vector.tensor_copy(v2w[0][:], tab2w[0][:].bitcast(U32).indirect(offs2_t[:]))
                if 1 <= k <= 4:
                    w, u = divmod(k - 1, 2)
                    for v in (2 * u, 2 * u + 1):
                        weave_w(w, 1, v * P // 4, (v + 1) * P // 4, WENG[4 * w + v])
                    if u == 1:
                        quant_w(w, 1, 0, PACK)
                if k == 3:
                    nc.vector.tensor_copy(v2w[1][:], tab2w[1][:].bitcast(U32).indirect(offs2_t[:]))
                if k == 5:
                    nc.vector.tensor_copy(v2s[:], tab2s[:].bitcast(U8).indirect(offs2_t[:]))
                finish(k - 2)
        for k in range(2 * last + 2 - 2, 2 * last + 2):
            finish(k)
        for job in range(2 * last + 2 - LAG, 2 * last):
            pick(job // 2, 1 - job % 2, 0, NP)
        half = NP // 2
        pick(last, 0, 0, half)
        weave_x(1, 0, 0, half, "scalar")
        pick(last, 1, 0, half)
        weave_x(1, 1, 0, half, "scalar")
        pick(last, 0, half, NP)
        pick(last, 1, half, NP)
        weave_x(1, 1, half, NP, "scalar")
        weave_x(1, 0, half, NP, "vector")
        quant_x(1, 0, 0, half)
        quant_x(1, 1, 0, half)
        quant_x(1, 0, half, NP)
        quant_x(1, 1, half, NP)

        tags = ("b0", "d0", "d1", "a1")
        acc = [psum.tile([P, 2, half], F32, name="acc%d" % g, tag=tags[g]) for g in range(4)]
        steps = ((0, 1), (0, 0), (1, 0), (1, 1))

        def second_stage(g, n):
            a, x = steps[n]
            ns = slice((g // 2) * half, (g // 2 + 1) * half)
            for u in range(2):
                j = 2 * (g % 2) + u
                cols = slice(j * P, (j + 1) * P)
                nc.tensor.matmul_mx(out=acc[g][:, u, :], lhsT=v2w[a][:, cols].bitcast(FP8X4), lhsT_scale=v2s[4 * a:P, cols],
                                    rhs=xq[a][x][:, ns].bitcast(FP8X4), rhs_scale=xs[a][x][:, ns],
                                    start=(n == 0 and u == 0), stop=(n == len(steps) - 1 and u == 1))

        for g in range(4):
            for n in range(2):
                second_stage(g, n)
        for g0 in (0, 2):
            for n in (2, 3):
                for g in (g0, g0 + 1):
                    second_stage(g, n)
        for g in range(4):
            res = held([P, 2, half], F32, "res%d" % g)
            for u in range(2):
                j = 2 * (g % 2) + u
                if g % 2 == 0:
                    nc.scalar.activation(res[:, u, :], acc[g][:, u, :], ACT.Identity, bias=prior_t[:, j:j + 1])
                else:
                    nc.vector.tensor_scalar(res[:, u, :], acc[g][:, u, :], prior_t[:, j:j + 1], None, ALU.add)
            rows = out[2 * (g % 2) * P:2 * (g % 2 + 1) * P, (g // 2) * half:(g // 2 + 1) * half]
            nc.sync.dma_start(out=rows.rearrange("(u p) n -> p u n", p=P), in_=res[:])
